import numpy as np
import ml_dtypes


def mxq(x, axis, fmt="e4m3"):
    dtype, down = {"e4m3": (ml_dtypes.float8_e4m3fn, 7), "e5m2": (ml_dtypes.float8_e5m2, 14)}[fmt]
    v = np.moveaxis(np.asarray(x, np.float32).astype(ml_dtypes.bfloat16).astype(np.float64), axis, -1)
    blocks = v.reshape(v.shape[:-1] + (-1, 32))
    amax = np.abs(blocks).max(-1, keepdims=True)
    byte = np.maximum(np.where(amax > 0, np.frexp(amax)[1] - 1 + 127, 0) - down, 1)
    scale = np.exp2(byte - 127.0)
    codes = (blocks / scale).astype(np.float32).astype(dtype).astype(np.float64)
    return np.moveaxis((codes * scale).reshape(v.shape), -1, axis)


WIDE = False


def mx_kscale(k):
    if not WIDE:
        return np.ones(k)
    levels = np.array([10, -10, 5, -5, 0])
    if k % 512:
        return np.exp2(np.random.permutation(np.resize(levels, k // 32))).repeat(32)
    a = np.empty((k // 512, 16))
    for p in range(k // 512):
        a[p, :8] = np.random.permutation(np.resize(levels, 8))
        for g in range(8):
            far = levels[np.abs(levels - a[p, g]) >= 10]
            a[p, g + 8] = far[np.random.randint(len(far))]
    return np.exp2(a.ravel()).repeat(32)


def f64(x):
    return np.asarray(x).astype(np.float64)


def striped(idx):
    return np.tile(idx.reshape(-1, 16).T, (8, 1)).astype(np.uint16)


def unstriped(offs):
    return offs[:16].T.reshape(-1).astype(np.int64)


E2M1 = np.array([0.0, 0.5, 1.0, 1.5, 2.0, 3.0, 4.0, 6.0, -0.0, -0.5, -1.0, -1.5, -2.0, -3.0, -4.0, -6.0])


def pack_weight(w, fmt):
    k, n = w.shape
    w = f64(np.asarray(w, np.float32).astype(ml_dtypes.bfloat16)).reshape(k // 32, 32, n)
    amax = np.abs(w).max(1)
    if fmt == "e4m3":
        byte = np.frexp(amax)[1] - 1 + 127 - 7
    else:
        mant, ex = np.frexp(amax / 6.0)
        byte = np.where(mant > 0.5, ex, ex - 1) + 127
    byte = np.clip(np.where(amax > 0, byte, 1), 1, 254)
    scaled = (w * np.exp2(127.0 - byte)[:, None, :]).reshape(k, n).astype(np.float32)
    by_word = np.ascontiguousarray(scaled.reshape(k // 512, 128, 4, n).transpose(0, 1, 3, 2))
    if fmt == "e4m3":
        words = by_word.astype(ml_dtypes.float8_e4m3fn).view(np.uint8)
    else:
        c = by_word.astype(ml_dtypes.float4_e2m1fn).view(np.uint8) & 0xF
        words = (c[..., 0::2] | (c[..., 1::2] << 4)).reshape(k // 512, 128, 2 * n)
    return np.ascontiguousarray(words), np.ascontiguousarray(byte.astype(np.uint8).reshape(k // 512, 16, n))


def unpack_weight(words, scales, fmt):
    g, _, n = scales.shape
    words = np.ascontiguousarray(words).reshape(g, 128, n, -1)
    if fmt == "e4m3":
        vals = words.view(ml_dtypes.float8_e4m3fn).astype(np.float64)
    else:
        nib = np.empty((g, 128, n, 4), np.uint8)
        nib[..., 0::2] = words & 0xF
        nib[..., 1::2] = words >> 4
        vals = E2M1[nib]
    vals = vals * np.repeat(np.exp2(scales.astype(np.float64) - 127.0), 8, axis=1)[..., None]
    return vals.transpose(0, 1, 3, 2).reshape(g * 512, n)


def gelu(v):
    return 0.5 * v * (1.0 + np.tanh(np.sqrt(2.0 / np.pi) * (v + 0.044715 * v**3)))


def bf(x):
    return np.asarray(x, np.float32).astype(ml_dtypes.bfloat16)


def planes(Y):
    n, m = Y.shape
    b = f64(bf(Y)).reshape(n // 32, 32, m)
    amax = np.abs(b).max(1)
    byte = np.clip(np.where(amax > 0, np.frexp(amax)[1] - 1 + 127 - 7, 1), 1, 254)
    codes = (b * np.exp2(127.0 - byte)[:, None, :]).reshape(n, m).astype(np.float32).astype(ml_dtypes.float8_e4m3fn).view(np.uint8)
    words = codes.reshape(n // 512, 128, 4, m).transpose(0, 1, 3, 2)
    return np.ascontiguousarray(words), np.ascontiguousarray(byte.astype(np.uint8).reshape(n // 512, 16, m))


K, T, S, H, T2, P, N = 1536, 4096, 1024, 512, 2048, 1024, 640

def setup_inputs():
    n = np.random.standard_normal
    s = mx_kscale(K)[:, None]
    u = mx_kscale(H)[:, None]
    d = {}
    d["tab_words"], d["tab_scales"] = pack_weight(n((K, T)) * s, "e4m3")
    d["offs"] = striped(np.random.permutation(T)[:S])
    d["offs2"] = striped(np.random.permutation(T2)[:S])
    d["offs3"] = striped(np.random.permutation(T2)[:P])
    d["w1"] = (1.5 * n((K, H)) / s / K ** 0.5).astype(np.float32)
    d["gain"] = (0.7 * np.sign(n(H)) * np.exp(0.3 * n(H)) * u[:, 0]).astype(np.float32)
    d["wgs"] = np.exp(0.3 * n((128, S))).astype(np.float32)
    d["page0"] = (n((H, T2)) * u).astype(np.float32)
    d["target"] = (n((H, P)) * u).astype(np.float32)
    d["w4_words"], d["w4_scales"] = pack_weight(1.2 * n((H, N)) / u / H ** 0.5, "e2m1")
    d["w3"] = (0.8 * n((K, N)) / s / K ** 0.5).astype(np.float32)
    return d

def reference(tab_words, tab_scales, offs, offs2, offs3, w1, gain, wgs, page0, target, w4_words, w4_scales, w3):
    v = unpack_weight(tab_words, tab_scales, "e4m3")[:, unstriped(offs)]
    w4 = unpack_weight(w4_words, w4_scales, "e2m1")
    strip = mxq(f64(w1), 0, "e4m3").T @ v
    h = f64(gain)[:, None] * np.sqrt(1.0 + np.square(strip))
    page = f64(page0).copy()
    page[:, unstriped(offs2)] = np.tile(f64(wgs), (H // 128, 1)) * h
    x = np.maximum(page[:, unstriped(offs3)], f64(target))
    xq = mxq(x, 0, "e4m3")
    w3q = mxq(f64(w3), 0, "e4m3")
    y = w4.T @ xq + w3q.T @ v
    words, scales = planes(page)
    return y, page, words, scales

@@ -1,0 +1,253 @@
+from contextlib import ExitStack
+
+import concourse.mybir as mybir
+from concourse.masks import make_identity
+
+K, T, S, H, T2, N = 1536, 4096, 1024, 512, 2048, 640
+FLOPS = 2 * K * H * S + 2 * H * N * S + 2 * K * N * S
+
+F32 = mybir.dt.float32
+BF16 = mybir.dt.bfloat16
+I32 = mybir.dt.int32
+U32 = mybir.dt.uint32
+U16 = mybir.dt.uint16
+U8 = mybir.dt.uint8
+FP8X4 = mybir.dt.float8_e4m3fn_x4
+FP4X4 = mybir.dt.float4_e2m1fn_x4
+ACT = mybir.ActivationFunctionType
+ALU = mybir.AluOpType
+
+P = 128
+PACK = 4
+PASSES = K // (P * PACK)
+BANK = 512
+HALVES = S // BANK
+BLOCKS = N // P
+
+
+def tile_list_mirror_zone_page_kernel(tc, tab_words, tab_scales, offs, offs2, offs3, w1, gain, wgs, page0,
+                                               target, w4_words, w4_scales, w3, out_0, out_1, out_2, out_3):
+    nc = tc.nc
+    with ExitStack() as ctx:
+        lists = ctx.enter_context(tc.tile_pool(name="lists", bufs=1))
+        sb = ctx.enter_context(tc.tile_pool(name="sb", bufs=1))
+        psum = ctx.enter_context(tc.psum_pool(name="psum", bufs=8))
+
+        def tile(shape, dtype, name, tag=None):
+            return sb.tile(shape, dtype, name=name, tag=tag or name, align_bytes=64)
+
+        def bank(name):
+            return psum.tile([P, BANK], F32, name=name, tag="bank")
+
+        def half(h):
+            return slice(h * BANK, (h + 1) * BANK)
+
+        def list_half(h):
+            return slice(h * BANK // 16, (h + 1) * BANK // 16)
+
+        ident = tile([P, P], F32, "ident")
+        make_identity(nc, ident[:])
+        tab_sc = tile([P, T], U8, "tab_sc")
+        nc.vector.memset(tab_sc[:].bitcast(I32), 0)
+        w4_sc = tile([P, N], U8, "w4_sc")
+        nc.vector.memset(w4_sc[:].bitcast(I32), 0)
+        one_in = tile([P, 1], F32, "one_in")
+        nc.vector.memset(one_in[:], 1.0)
+        one = tile([P, 1], F32, "one")
+        nc.scalar.activation(one[:], one_in[:], ACT.Sqrt)
+
+        wgs_sb = tile([P, S], F32, "wgs_sb")
+        nc.sync.dma_start(wgs_sb[:], wgs)
+        idx = lists.tile([P, S // 16], U16, name="idx")
+        nc.sync.dma_start(idx[:], offs)
+        gain_sb = tile([P, PACK], F32, "gain_sb")
+        nc.sync.dma_start(gain_sb[:], gain.rearrange("(p t) -> p t", t=PACK))
+        idx2 = lists.tile([P, S // 16], U16, name="idx2")
+        nc.sync.dma_start(idx2[:], offs2)
+        idx3 = lists.tile([P, S // 16], U16, name="idx3")
+        nc.sync.dma_start(idx3[:], offs3)
+        w4_codes = tile([P, 2 * N], U8, "w4_codes")
+        nc.sync.dma_start(w4_codes[:].bitcast(I32), w4_words[0].bitcast(I32))
+        tab = []
+        w1_raw = []
+        for a in range(PASSES):
+            words = tile([P, T], I32, f"tab{a}", tag=f"wide{a}")
+            nc.sync.dma_start(words[:], tab_words[a].rearrange("p n t -> p (n t)").bitcast(I32))
+            tab.append(words)
+            if a == 0:
+                for q in range(4):
+                    nc.sync.dma_start(tab_sc[32 * q : 32 * q + 4 * PASSES, :].bitcast(I32),
+                                      tab_scales[:, 4 * q : 4 * q + 4, :].bitcast(I32))
+            raw = tile([P, PACK, H], F32, f"w1_raw{a}", tag=f"mid{a}")
+            nc.sync.dma_start(raw[:], w1[a * 512 : (a + 1) * 512, :].rearrange("(p j) c -> p j c", j=PACK))
+            w1_raw.append(raw)
+        page_rows = page0.rearrange("(p t) c -> t p c", t=PACK)
+        page = [tile([P, T2], F32, f"page{t}") for t in range(PACK)]
+        w3_raw = [tile([P, PACK, N], F32, f"w3_raw{a}", tag=f"ten{a}") for a in range(PASSES - 1)]
+
+        wgs_t = tile([P, PACK * S], F32, "wgs_t", tag="spare")
+        wgs_t5 = wgs_t[:].rearrange("j (b t r q) -> j b t r q", t=PACK, r=4, q=32)
+        for h in range(HALVES):
+            turned = bank("turned")
+            for b in range(4):
+                nc.tensor.transpose(turned[:, b * P : (b + 1) * P], wgs_sb[:, (4 * h + b) * P : (4 * h + b + 1) * P], ident[:])
+            src = turned[:].rearrange("j (b q t) -> j b t q", t=PACK, q=32).unsqueeze(3).to_broadcast([P, 4, PACK, 4, 32])
+            if h == 0:
+                nc.scalar.copy(wgs_t5[:, 4 * h : 4 * h + 4], src)
+            else:
+                nc.vector.tensor_copy(wgs_t5[:, 4 * h : 4 * h + 4], src)
+        factor = tile([P, PACK * S], F32, "factor")
+        for t in range(PACK):
+            for h in range(HALVES):
+                back = bank("back")
+                for b in range(4):
+                    start = ((4 * h + b) * PACK + t) * P
+                    nc.tensor.transpose(back[:, b * P : (b + 1) * P], wgs_t[:, start : start + P], ident[:])
+                nc.scalar.activation(factor[:, t * S + h * BANK : t * S + (h + 1) * BANK], back[:], ACT.Copy,
+                                     scale=gain_sb[:, t : t + 1])
+
+        v = []
+        v_sc = tile([P, S], U8, "v_sc")
+        strips = [[bank(f"strip{t}{h}") for h in range(HALVES)] for t in range(PACK)]
+        for a in range(PASSES):
+            picked = tile([P, S], U32, f"v{a}")
+            nc.vector.tensor_copy(picked[:], tab[a][:].bitcast(U32).indirect(idx[:]))
+            v.append(picked)
+            if a == 0:
+                nc.vector.tensor_copy(v_sc[:], tab_sc[:].indirect(idx[:]))
+            for u in range(2):
+                grouped = tile([P, 2 * P * PACK], BF16, f"w1_bf{a}{u}")
+                dst = grouped[:].rearrange("p (e m j) -> p m j e", e=2, j=PACK)
+                src = w1_raw[a][:].rearrange("p j (m u e) -> p u m j e", u=2, e=2)[:, u]
+                if u == 0:
+                    nc.vector.tensor_copy(dst, src)
+                else:
+                    nc.scalar.copy(dst, src)
+                codes = tile([P, 2 * P], U32, f"w1_codes{a}{u}")
+                scales = tile([P, 2 * P], U8, f"w1_sc{a}{u}")
+                nc.vector.quantize_mx(out=codes[:].bitcast(FP8X4), scales=scales[:], in_=grouped[:])
+                for e in range(2):
+                    for h in range(HALVES):
+                        nc.tensor.matmul_mx(out=strips[2 * u + e][h][:],
+                                            lhsT=codes[:, e * P : (e + 1) * P].bitcast(FP8X4),
+                                            lhsT_scale=scales[:, e * P : (e + 1) * P],
+                                            rhs=v[a][:, half(h)].bitcast(FP8X4), rhs_scale=v_sc[4 * a : P, half(h)],
+                                            start=(a == 0), stop=(a == PASSES - 1))
+
+        w3_raw.append(tile([P, PACK, N], F32, "w3_raw2", tag="wide1"))
+        target_sb = tile([P, PACK, S], F32, "target_sb", tag="wide0")
+
+        def load_w3(a):
+            nc.sync.dma_start(w3_raw[a][:], w3[a * 512 : (a + 1) * 512, :].rearrange("(p j) c -> p j c", j=PACK))
+
+        nc.sync.dma_start(page[0][:], page_rows[0])
+        nc.sync.dma_start(page[1][:], page_rows[1])
+        load_w3(0)
+        nc.sync.dma_start(page[2][:], page_rows[2])
+        load_w3(1)
+        for q in range(4):
+            nc.sync.dma_start(w4_sc[32 * q : 32 * q + 4, :].bitcast(I32), w4_scales[0, 4 * q : 4 * q + 4, :].bitcast(I32))
+        nc.sync.dma_start(target_sb[:], target.rearrange("(p t) j -> p t j", t=PACK))
+        nc.sync.dma_start(page[3][:], page_rows[3])
+        load_w3(2)
+
+        root = tile([P, PACK * S], F32, "root", tag="wide2")
+        page_out = out_1.rearrange("(p t) c -> t p c", t=PACK)
+        for t in range(PACK):
+            pieces = [slice(t * S + h * BANK, t * S + (h + 1) * BANK) for h in range(HALVES)]
+            for h in range(HALVES):
+                nc.scalar.activation(root[:, pieces[h]], strips[t][h][:], ACT.Square)
+                nc.scalar.activation(root[:, pieces[h]], root[:, pieces[h]], ACT.Sqrt, bias=one[:])
+            if t == 0:
+                for h in range(HALVES):
+                    nc.vector.tensor_tensor(page[t][:].indirect(idx2[:, list_half(h)]), root[:, pieces[h]],
+                                            factor[:, pieces[h]], ALU.mult)
+            else:
+                whole = slice(t * S, (t + 1) * S)
+                nc.vector.tensor_tensor(page[t][:].indirect(idx2[:]), root[:, whole], factor[:, whole], ALU.mult)
+            nc.sync.dma_start(page_out[t], page[t][:])
+
+        w3_bf = tile([P, PASSES * N * PACK], BF16, "w3_bf", tag="spare")
+        w3_codes = tile([P, PASSES * N], U32, "w3_codes")
+        w3_sc = tile([P, PASSES * N], U8, "w3_sc")
+        for a in range(PASSES):
+            dst = w3_bf[:, a * N * PACK : (a + 1) * N * PACK].rearrange("p (c i j) -> p c j i", i=2, j=PACK)
+            nc.scalar.copy(dst, w3_raw[a][:].rearrange("p j (c i) -> p c j i", i=2))
+            for c0, c1 in ((a * N, a * N + 512), (a * N + 512, (a + 1) * N)):
+                nc.vector.quantize_mx(out=w3_codes[:, c0:c1].bitcast(FP8X4), scales=w3_sc[:, c0:c1],
+                                      in_=w3_bf[:, c0 * PACK : c1 * PACK])
+
+        def strip_passes(acc, b, h):
+            for a in range(PASSES):
+                cols = slice(a * N + b * P, a * N + (b + 1) * P)
+                nc.tensor.matmul_mx(out=acc[:], lhsT=w3_codes[:, cols].bitcast(FP8X4), lhsT_scale=w3_sc[:, cols],
+                                    rhs=v[a][:, half(h)].bitcast(FP8X4), rhs_scale=v_sc[4 * a : P, half(h)],
+                                    start=(a == 0), stop=False)
+
+        order = [(h, b) for h in range(HALVES) for b in range(BLOCKS)]
+        acc = {}
+        for h, b in order[:8]:
+            acc[h, b] = bank(f"y{h}{b}")
+            strip_passes(acc[h, b], b, h)
+
+        pairs = tile([P, PACK * T2], BF16, "pairs", tag="wide1")
+        pairs4 = pairs[:].rearrange("p (u c e) -> p u e c", u=2, e=2)
+        for t in range(PACK):
+            nc.scalar.copy(pairs4[:, t // 2, t % 2], page[t][:])
+        woven = tile([P, 2 * T2], F32, "woven", tag="wide2")
+        pair_words = pairs[:].bitcast(F32).rearrange("p (u c) -> p c u", u=2)
+        for h in range(2):
+            cols = slice(h * T2 // 2, (h + 1) * T2 // 2)
+            nc.scalar.copy(woven[:, h * T2 : (h + 1) * T2].rearrange("p (c u) -> p c u", u=2), pair_words[:, cols])
+
+        zones = tile([P, PACK * S], F32, "zones", tag="spare")
+        x_codes = tile([P, S], U32, "x_codes")
+        x_sc = tile([P, S], U8, "x_sc")
+        def fetch(h, t):
+            c0 = (h * PACK + t) * BANK
+            nc.vector.tensor_copy(zones[:, c0 : c0 + BANK], page[t][:].indirect(idx3[:, list_half(h)]))
+
+        def larger(h):
+            x_bf = tile([P, BANK * PACK], BF16, f"x_bf{h}", tag=f"mid{h}")
+            nc.vector.tensor_tensor(
+                x_bf[:].rearrange("p (c i t) -> p c t i", i=2, t=PACK),
+                zones[:, h * PACK * BANK : (h + 1) * PACK * BANK].rearrange("p (t c i) -> p c t i", i=2, t=PACK),
+                target_sb[:, :, half(h)].rearrange("p t (c i) -> p c t i", i=2),
+                ALU.max)
+            return x_bf
+
+        def finish(h, x_bf):
+            nc.vector.quantize_mx(out=x_codes[:, half(h)].bitcast(FP8X4), scales=x_sc[:, half(h)], in_=x_bf[:])
+            y_sb = tile([P, BLOCKS, BANK], F32, f"y_sb{h}", tag=f"ten{h}")
+            for b in range(BLOCKS):
+                if (h, b) not in acc:
+                    acc[h, b] = bank(f"y{h}{b}")
+                    strip_passes(acc[h, b], b, h)
+            for b in range(BLOCKS):
+                nc.tensor.matmul_mx(out=acc[h, b][:], lhsT=w4_codes[:, 2 * b * P : 2 * (b + 1) * P].bitcast(FP4X4),
+                                    lhsT_scale=w4_sc[:, b * P : (b + 1) * P],
+                                    rhs=x_codes[:, half(h)].bitcast(FP8X4), rhs_scale=x_sc[:, half(h)],
+                                    start=False, stop=True)
+                nc.scalar.copy(y_sb[:, b, :], acc[h, b][:])
+                nc.sync.dma_start(out_0[b * P : (b + 1) * P, half(h)], y_sb[:, b, :])
+
+        for t in range(PACK):
+            fetch(0, t)
+        fetch(1, 0)
+        first = larger(0)
+        fetch(1, 1)
+        finish(0, first)
+        fetch(1, 2)
+        fetch(1, 3)
+        finish(1, larger(1))
+
+        plane_codes = tile([P, T2], U32, "plane_codes", tag="mid1")
+        plane_sc = tile([P, T2], U8, "plane_sc")
+        words_out = out_2[0].rearrange("p m t -> p (m t)").bitcast(I32)
+        for h in range(2):
+            cols = slice(h * T2 // 2, (h + 1) * T2 // 2)
+            nc.vector.quantize_mx(out=plane_codes[:, cols].bitcast(FP8X4), scales=plane_sc[:, cols],
+                                  in_=woven[:, h * T2 : (h + 1) * T2].bitcast(BF16))
+            nc.sync.dma_start(words_out[:, cols], plane_codes[:, cols].bitcast(I32))
+        for q in range(4):
+            nc.sync.dma_start(out_3[0, 4 * q : 4 * q + 4, :].bitcast(I32), plane_sc[32 * q : 32 * q + 4, :].bitcast(I32))

@@ -23,6 +23,7 @@ PASSES = K // (P * PACK)
 BANK = 512
 HALVES = S // BANK
 BLOCKS = N // P
+EARLY = 3
 
 
 def tile_list_mirror_zone_page_kernel(tc, tab_words, tab_scales, offs, offs2, offs3, w1, gain, wgs, page0,
@@ -31,13 +32,13 @@ def tile_list_mirror_zone_page_kernel(tc, tab_words, tab_scales, offs, offs2, of
     with ExitStack() as ctx:
         lists = ctx.enter_context(tc.tile_pool(name="lists", bufs=1))
         sb = ctx.enter_context(tc.tile_pool(name="sb", bufs=1))
-        psum = ctx.enter_context(tc.psum_pool(name="psum", bufs=8))
+        psum = ctx.enter_context(tc.psum_pool(name="psum", bufs=1))
 
         def tile(shape, dtype, name, tag=None):
             return sb.tile(shape, dtype, name=name, tag=tag or name, align_bytes=64)
 
-        def bank(name):
-            return psum.tile([P, BANK], F32, name=name, tag="bank")
+        def bank(name, n):
+            return psum.tile([P, BANK], F32, name=name, tag=f"bank{n}")
 
         def half(h):
             return slice(h * BANK, (h + 1) * BANK)
@@ -56,8 +57,9 @@ def tile_list_mirror_zone_page_kernel(tc, tab_words, tab_scales, offs, offs2, of
         one = tile([P, 1], F32, "one")
         nc.scalar.activation(one[:], one_in[:], ACT.Sqrt)
 
-        wgs_sb = tile([P, S], F32, "wgs_sb")
-        nc.sync.dma_start(wgs_sb[:], wgs)
+        wgs_sb = [tile([P, BANK], F32, f"wgs_sb{h}") for h in range(HALVES)]
+        for h in range(HALVES):
+            nc.sync.dma_start(wgs_sb[h][:], wgs[:, half(h)])
         idx = lists.tile([P, S // 16], U16, name="idx")
         nc.sync.dma_start(idx[:], offs)
         gain_sb = tile([P, PACK], F32, "gain_sb")
@@ -66,8 +68,6 @@ def tile_list_mirror_zone_page_kernel(tc, tab_words, tab_scales, offs, offs2, of
         nc.sync.dma_start(idx2[:], offs2)
         idx3 = lists.tile([P, S // 16], U16, name="idx3")
         nc.sync.dma_start(idx3[:], offs3)
-        w4_codes = tile([P, 2 * N], U8, "w4_codes")
-        nc.sync.dma_start(w4_codes[:].bitcast(I32), w4_words[0].bitcast(I32))
         tab = []
         w1_raw = []
         for a in range(PASSES):
@@ -88,9 +88,9 @@ def tile_list_mirror_zone_page_kernel(tc, tab_words, tab_scales, offs, offs2, of
         wgs_t = tile([P, PACK * S], F32, "wgs_t", tag="spare")
         wgs_t5 = wgs_t[:].rearrange("j (b t r q) -> j b t r q", t=PACK, r=4, q=32)
         for h in range(HALVES):
-            turned = bank("turned")
+            turned = bank("turned", h)
             for b in range(4):
-                nc.tensor.transpose(turned[:, b * P : (b + 1) * P], wgs_sb[:, (4 * h + b) * P : (4 * h + b + 1) * P], ident[:])
+                nc.tensor.transpose(turned[:, b * P : (b + 1) * P], wgs_sb[h][:, b * P : (b + 1) * P], ident[:])
             src = turned[:].rearrange("j (b q t) -> j b t q", t=PACK, q=32).unsqueeze(3).to_broadcast([P, 4, PACK, 4, 32])
             if h == 0:
                 nc.scalar.copy(wgs_t5[:, 4 * h : 4 * h + 4], src)
@@ -99,7 +99,7 @@ def tile_list_mirror_zone_page_kernel(tc, tab_words, tab_scales, offs, offs2, of
         factor = tile([P, PACK * S], F32, "factor")
         for t in range(PACK):
             for h in range(HALVES):
-                back = bank("back")
+                back = bank("back", (2 + HALVES * t + h) % 8)
                 for b in range(4):
                     start = ((4 * h + b) * PACK + t) * P
                     nc.tensor.transpose(back[:, b * P : (b + 1) * P], wgs_t[:, start : start + P], ident[:])
@@ -108,7 +108,7 @@ def tile_list_mirror_zone_page_kernel(tc, tab_words, tab_scales, offs, offs2, of
 
         v = []
         v_sc = tile([P, S], U8, "v_sc")
-        strips = [[bank(f"strip{t}{h}") for h in range(HALVES)] for t in range(PACK)]
+        strips = [[bank(f"strip{t}{h}", (2 + HALVES * t + h) % 8) for h in range(HALVES)] for t in range(PACK)]
         for a in range(PASSES):
             picked = tile([P, S], U32, f"v{a}")
             nc.vector.tensor_copy(picked[:], tab[a][:].bitcast(U32).indirect(idx[:]))
@@ -140,16 +140,15 @@ def tile_list_mirror_zone_page_kernel(tc, tab_words, tab_scales, offs, offs2, of
         def load_w3(a):
             nc.sync.dma_start(w3_raw[a][:], w3[a * 512 : (a + 1) * 512, :].rearrange("(p j) c -> p j c", j=PACK))
 
-        nc.sync.dma_start(page[0][:], page_rows[0])
-        nc.sync.dma_start(page[1][:], page_rows[1])
-        load_w3(0)
-        nc.sync.dma_start(page[2][:], page_rows[2])
-        load_w3(1)
+        for a in range(PASSES):
+            nc.sync.dma_start(page[a][:], page_rows[a])
+            load_w3(a)
+        nc.sync.dma_start(page[PASSES][:], page_rows[PASSES])
+        w4_codes = tile([P, 2 * N], U8, "w4_codes")
+        nc.sync.dma_start(w4_codes[:].bitcast(I32), w4_words[0].bitcast(I32))
         for q in range(4):
             nc.sync.dma_start(w4_sc[32 * q : 32 * q + 4, :].bitcast(I32), w4_scales[0, 4 * q : 4 * q + 4, :].bitcast(I32))
         nc.sync.dma_start(target_sb[:], target.rearrange("(p t) j -> p t j", t=PACK))
-        nc.sync.dma_start(page[3][:], page_rows[3])
-        load_w3(2)
 
         root = tile([P, PACK * S], F32, "root", tag="wide2")
         page_out = out_1.rearrange("(p t) c -> t p c", t=PACK)
@@ -184,70 +183,80 @@ def tile_list_mirror_zone_page_kernel(tc, tab_words, tab_scales, offs, offs2, of
                                     rhs=v[a][:, half(h)].bitcast(FP8X4), rhs_scale=v_sc[4 * a : P, half(h)],
                                     start=(a == 0), stop=False)
 
-        order = [(h, b) for h in range(HALVES) for b in range(BLOCKS)]
-        acc = {}
-        for h, b in order[:8]:
-            acc[h, b] = bank(f"y{h}{b}")
-            strip_passes(acc[h, b], b, h)
+        def open_sums(h, blocks):
+            sums = [bank(f"y{h}{b}", b) for b in blocks]
+            for acc, b in zip(sums, blocks):
+                strip_passes(acc, b, h)
+            return sums
+
+        first_sums = open_sums(0, range(BLOCKS))
 
         pairs = tile([P, PACK * T2], BF16, "pairs", tag="wide1")
         pairs4 = pairs[:].rearrange("p (u c e) -> p u e c", u=2, e=2)
         for t in range(PACK):
             nc.scalar.copy(pairs4[:, t // 2, t % 2], page[t][:])
-        woven = tile([P, 2 * T2], F32, "woven", tag="wide2")
-        pair_words = pairs[:].bitcast(F32).rearrange("p (u c) -> p c u", u=2)
+        pair_words = pairs[:].bitcast(F32).rearrange("p (u c i) -> p c u i", u=2, i=2)
+        woven = []
         for h in range(2):
-            cols = slice(h * T2 // 2, (h + 1) * T2 // 2)
-            nc.scalar.copy(woven[:, h * T2 : (h + 1) * T2].rearrange("p (c u) -> p c u", u=2), pair_words[:, cols])
+            part = tile([P, T2], F32, f"woven{h}", tag=f"mid{h + 1}")
+            nc.scalar.copy(part[:].rearrange("p (c i u) -> p c u i", u=2, i=2),
+                           pair_words[:, h * T2 // 4 : (h + 1) * T2 // 4])
+            woven.append(part)
 
-        zones = tile([P, PACK * S], F32, "zones", tag="spare")
         x_codes = tile([P, S], U32, "x_codes")
         x_sc = tile([P, S], U8, "x_sc")
-        def fetch(h, t):
-            c0 = (h * PACK + t) * BANK
-            nc.vector.tensor_copy(zones[:, c0 : c0 + BANK], page[t][:].indirect(idx3[:, list_half(h)]))
 
-        def larger(h):
-            x_bf = tile([P, BANK * PACK], BF16, f"x_bf{h}", tag=f"mid{h}")
+        def fetch(zones, h, t):
+            nc.vector.tensor_copy(zones[:, t * BANK : (t + 1) * BANK], page[t][:].indirect(idx3[:, list_half(h)]))
+
+        def larger(zones, h, tag):
+            x_bf = tile([P, BANK * PACK], BF16, f"x_bf{h}", tag=tag)
             nc.vector.tensor_tensor(
                 x_bf[:].rearrange("p (c i t) -> p c t i", i=2, t=PACK),
-                zones[:, h * PACK * BANK : (h + 1) * PACK * BANK].rearrange("p (t c i) -> p c t i", i=2, t=PACK),
+                zones[:].rearrange("p (t c i) -> p c t i", i=2, t=PACK),
                 target_sb[:, :, half(h)].rearrange("p t (c i) -> p c t i", i=2),
                 ALU.max)
             return x_bf
 
-        def finish(h, x_bf):
+        def close_sums(sums, h, x_bf):
             nc.vector.quantize_mx(out=x_codes[:, half(h)].bitcast(FP8X4), scales=x_sc[:, half(h)], in_=x_bf[:])
-            y_sb = tile([P, BLOCKS, BANK], F32, f"y_sb{h}", tag=f"ten{h}")
             for b in range(BLOCKS):
-                if (h, b) not in acc:
-                    acc[h, b] = bank(f"y{h}{b}")
-                    strip_passes(acc[h, b], b, h)
-            for b in range(BLOCKS):
-                nc.tensor.matmul_mx(out=acc[h, b][:], lhsT=w4_codes[:, 2 * b * P : 2 * (b + 1) * P].bitcast(FP4X4),
+                nc.tensor.matmul_mx(out=sums[b][:], lhsT=w4_codes[:, 2 * b * P : 2 * (b + 1) * P].bitcast(FP4X4),
                                     lhsT_scale=w4_sc[:, b * P : (b + 1) * P],
                                     rhs=x_codes[:, half(h)].bitcast(FP8X4), rhs_scale=x_sc[:, half(h)],
                                     start=False, stop=True)
-                nc.scalar.copy(y_sb[:, b, :], acc[h, b][:])
-                nc.sync.dma_start(out_0[b * P : (b + 1) * P, half(h)], y_sb[:, b, :])
 
+        def hand_out(sums, h, blocks, tag, copies):
+            y_sb = tile([P, len(blocks), BANK], F32, f"y_sb{h}{blocks[0]}", tag=tag)
+            for n, b in enumerate(blocks):
+                copies[n % len(copies)](y_sb[:, n, :], sums[b][:])
+                nc.sync.dma_start(out_0[b * P : (b + 1) * P, half(h)], y_sb[:, n, :])
+
+        zones_a = tile([P, PACK * BANK], F32, "zones_a", tag="spare")
         for t in range(PACK):
-            fetch(0, t)
-        fetch(1, 0)
-        first = larger(0)
-        fetch(1, 1)
-        finish(0, first)
-        fetch(1, 2)
-        fetch(1, 3)
-        finish(1, larger(1))
+            fetch(zones_a, 0, t)
+        x_a = larger(zones_a, 0, "mid0")
+        zones_b = tile([P, PACK * BANK], F32, "zones_b", tag="spare")
+        fetch(zones_b, 1, 0)
+        close_sums(first_sums, 0, x_a)
+        hand_out(first_sums, 0, range(EARLY), "ten0", [nc.scalar.copy])
+        second_sums = open_sums(1, range(EARLY))
+        for t in range(1, PACK):
+            fetch(zones_b, 1, t)
 
-        plane_codes = tile([P, T2], U32, "plane_codes", tag="mid1")
+        plane_codes = tile([P, T2], U32, "plane_codes")
         plane_sc = tile([P, T2], U8, "plane_sc")
         words_out = out_2[0].rearrange("p m t -> p (m t)").bitcast(I32)
         for h in range(2):
             cols = slice(h * T2 // 2, (h + 1) * T2 // 2)
             nc.vector.quantize_mx(out=plane_codes[:, cols].bitcast(FP8X4), scales=plane_sc[:, cols],
-                                  in_=woven[:, h * T2 : (h + 1) * T2].bitcast(BF16))
+                                  in_=woven[h][:].bitcast(BF16))
             nc.sync.dma_start(words_out[:, cols], plane_codes[:, cols].bitcast(I32))
+            if h == 0:
+                hand_out(first_sums, 0, range(EARLY, BLOCKS), "mid1", [nc.scalar.copy])
+                second_sums = second_sums + open_sums(1, range(EARLY, BLOCKS))
         for q in range(4):
             nc.sync.dma_start(out_3[0, 4 * q : 4 * q + 4, :].bitcast(I32), plane_sc[32 * q : 32 * q + 4, :].bitcast(I32))
+
+        close_sums(second_sums, 1, larger(zones_b, 1, "mid2"))
+        hand_out(second_sums, 1, range(BLOCKS), "ten1", [nc.scalar.copy, nc.vector.tensor_copy])

@@ -23,7 +23,8 @@ PASSES = K // (P * PACK)
 BANK = 512
 HALVES = S // BANK
 BLOCKS = N // P
-EARLY = 3
+LEAD = 256
+PIECES = ((0, 512), (512, 256), (768, 256))
 
 
 def tile_list_mirror_zone_page_kernel(tc, tab_words, tab_scales, offs, offs2, offs3, w1, gain, wgs, page0,
@@ -108,7 +109,18 @@ def tile_list_mirror_zone_page_kernel(tc, tab_words, tab_scales, offs, offs2, of
 
         v = []
         v_sc = tile([P, S], U8, "v_sc")
-        strips = [[bank(f"strip{t}{h}", (2 + HALVES * t + h) % 8) for h in range(HALVES)] for t in range(PACK)]
+        groups = [(0, 0, LEAD), (0, LEAD, BANK - LEAD)] + [(t, h * BANK, BANK) for t in range(PACK) for h in range(HALVES)][1:]
+        strips = {group: bank(f"strip{n}", (2 + n) % 8) for n, group in enumerate(groups[:8])}
+        w1_q = {}
+
+        def strip_pass(group, a):
+            t, c0, width = group
+            codes, scales = w1_q[a, t // 2]
+            cols = slice(t % 2 * P, (t % 2 + 1) * P)
+            nc.tensor.matmul_mx(out=strips[group][:, 0:width], lhsT=codes[:, cols].bitcast(FP8X4), lhsT_scale=scales[:, cols],
+                                rhs=v[a][:, c0 : c0 + width].bitcast(FP8X4), rhs_scale=v_sc[4 * a : P, c0 : c0 + width],
+                                start=(a == 0), stop=(a == PASSES - 1))
+
         for a in range(PASSES):
             picked = tile([P, S], U32, f"v{a}")
             nc.vector.tensor_copy(picked[:], tab[a][:].bitcast(U32).indirect(idx[:]))
@@ -126,13 +138,10 @@ def tile_list_mirror_zone_page_kernel(tc, tab_words, tab_scales, offs, offs2, of
                 codes = tile([P, 2 * P], U32, f"w1_codes{a}{u}")
                 scales = tile([P, 2 * P], U8, f"w1_sc{a}{u}")
                 nc.vector.quantize_mx(out=codes[:].bitcast(FP8X4), scales=scales[:], in_=grouped[:])
-                for e in range(2):
-                    for h in range(HALVES):
-                        nc.tensor.matmul_mx(out=strips[2 * u + e][h][:],
-                                            lhsT=codes[:, e * P : (e + 1) * P].bitcast(FP8X4),
-                                            lhsT_scale=scales[:, e * P : (e + 1) * P],
-                                            rhs=v[a][:, half(h)].bitcast(FP8X4), rhs_scale=v_sc[4 * a : P, half(h)],
-                                            start=(a == 0), stop=(a == PASSES - 1))
+                w1_q[a, u] = (codes, scales)
+                for group in groups[:8]:
+                    if group[0] // 2 == u:
+                        strip_pass(group, a)
 
         w3_raw.append(tile([P, PACK, N], F32, "w3_raw2", tag="wide1"))
         target_sb = tile([P, PACK, S], F32, "target_sb", tag="wide0")
@@ -153,15 +162,19 @@ def tile_list_mirror_zone_page_kernel(tc, tab_words, tab_scales, offs, offs2, of
         root = tile([P, PACK * S], F32, "root", tag="wide2")
         page_out = out_1.rearrange("(p t) c -> t p c", t=PACK)
         for t in range(PACK):
-            pieces = [slice(t * S + h * BANK, t * S + (h + 1) * BANK) for h in range(HALVES)]
-            for h in range(HALVES):
-                nc.scalar.activation(root[:, pieces[h]], strips[t][h][:], ACT.Square)
-                nc.scalar.activation(root[:, pieces[h]], root[:, pieces[h]], ACT.Sqrt, bias=one[:])
-            if t == 0:
-                for h in range(HALVES):
-                    nc.vector.tensor_tensor(page[t][:].indirect(idx2[:, list_half(h)]), root[:, pieces[h]],
-                                            factor[:, pieces[h]], ALU.mult)
-            else:
+            for group in [group for group in groups if group[0] == t]:
+                c0, width = group[1:]
+                cols = slice(t * S + c0, t * S + c0 + width)
+                nc.scalar.activation(root[:, cols], strips[group][:, 0:width], ACT.Square)
+                nc.scalar.activation(root[:, cols], root[:, cols], ACT.Sqrt, bias=one[:])
+                if group == groups[0]:
+                    strips[groups[8]] = bank("strip8", 2)
+                    for a in range(PASSES):
+                        strip_pass(groups[8], a)
+                if t == 0:
+                    nc.vector.tensor_tensor(page[t][:].indirect(idx2[:, c0 // 16 : (c0 + width) // 16]), root[:, cols],
+                                            factor[:, cols], ALU.mult)
+            if t > 0:
                 whole = slice(t * S, (t + 1) * S)
                 nc.vector.tensor_tensor(page[t][:].indirect(idx2[:]), root[:, whole], factor[:, whole], ALU.mult)
             nc.sync.dma_start(page_out[t], page[t][:])
@@ -176,20 +189,26 @@ def tile_list_mirror_zone_page_kernel(tc, tab_words, tab_scales, offs, offs2, of
                 nc.vector.quantize_mx(out=w3_codes[:, c0:c1].bitcast(FP8X4), scales=w3_sc[:, c0:c1],
                                       in_=w3_bf[:, c0 * PACK : c1 * PACK])
 
-        def strip_passes(acc, b, h):
-            for a in range(PASSES):
-                cols = slice(a * N + b * P, a * N + (b + 1) * P)
-                nc.tensor.matmul_mx(out=acc[:], lhsT=w3_codes[:, cols].bitcast(FP8X4), lhsT_scale=w3_sc[:, cols],
-                                    rhs=v[a][:, half(h)].bitcast(FP8X4), rhs_scale=v_sc[4 * a : P, half(h)],
-                                    start=(a == 0), stop=False)
+        def bank_plan(c0, width):
+            per_bank = BANK // width
+            return [(c0, width, list(range(b, min(b + per_bank, BLOCKS)))) for b in range(0, BLOCKS, per_bank)]
 
-        def open_sums(h, blocks):
-            sums = [bank(f"y{h}{b}", b) for b in blocks]
-            for acc, b in zip(sums, blocks):
-                strip_passes(acc, b, h)
-            return sums
+        def open_sum(plan, n):
+            c0, width, blocks = plan
+            acc = bank(f"y{c0}_{blocks[0]}", n)
+            for place, b in enumerate(blocks):
+                for a in range(PASSES):
+                    cols = slice(a * N + b * P, a * N + (b + 1) * P)
+                    nc.tensor.matmul_mx(out=acc[:, place * width : (place + 1) * width],
+                                        lhsT=w3_codes[:, cols].bitcast(FP8X4), lhsT_scale=w3_sc[:, cols],
+                                        rhs=v[a][:, c0 : c0 + width].bitcast(FP8X4),
+                                        rhs_scale=v_sc[4 * a : P, c0 : c0 + width],
+                                        start=(place == 0 and a == 0), stop=False)
+            return acc
 
-        first_sums = open_sums(0, range(BLOCKS))
+        plans = [bank_plan(c0, width) for c0, width in PIECES]
+        sums = [[open_sum(plan, n) for n, plan in enumerate(plans[0])]]
+        sums.append([open_sum(plan, len(plans[0]) + n) for n, plan in enumerate(plans[1])])
 
         pairs = tile([P, PACK * T2], BF16, "pairs", tag="wide1")
         pairs4 = pairs[:].rearrange("p (u c e) -> p u e c", u=2, e=2)
@@ -206,57 +225,69 @@ def tile_list_mirror_zone_page_kernel(tc, tab_words, tab_scales, offs, offs2, of
         x_codes = tile([P, S], U32, "x_codes")
         x_sc = tile([P, S], U8, "x_sc")
 
-        def fetch(zones, h, t):
-            nc.vector.tensor_copy(zones[:, t * BANK : (t + 1) * BANK], page[t][:].indirect(idx3[:, list_half(h)]))
+        def fetch(zones, c0, width, t):
+            nc.vector.tensor_copy(zones[:, t * width : (t + 1) * width],
+                                  page[t][:].indirect(idx3[:, c0 // 16 : (c0 + width) // 16]))
 
-        def larger(zones, h, tag):
-            x_bf = tile([P, BANK * PACK], BF16, f"x_bf{h}", tag=tag)
+        def larger(zones, c0, width, tag):
+            x_bf = tile([P, width * PACK], BF16, f"x_bf{c0}", tag=tag)
             nc.vector.tensor_tensor(
                 x_bf[:].rearrange("p (c i t) -> p c t i", i=2, t=PACK),
                 zones[:].rearrange("p (t c i) -> p c t i", i=2, t=PACK),
-                target_sb[:, :, half(h)].rearrange("p t (c i) -> p c t i", i=2),
+                target_sb[:, :, c0 : c0 + width].rearrange("p t (c i) -> p c t i", i=2),
                 ALU.max)
             return x_bf
 
-        def close_sums(sums, h, x_bf):
-            nc.vector.quantize_mx(out=x_codes[:, half(h)].bitcast(FP8X4), scales=x_sc[:, half(h)], in_=x_bf[:])
-            for b in range(BLOCKS):
-                nc.tensor.matmul_mx(out=sums[b][:], lhsT=w4_codes[:, 2 * b * P : 2 * (b + 1) * P].bitcast(FP4X4),
-                                    lhsT_scale=w4_sc[:, b * P : (b + 1) * P],
-                                    rhs=x_codes[:, half(h)].bitcast(FP8X4), rhs_scale=x_sc[:, half(h)],
-                                    start=False, stop=True)
-
-        def hand_out(sums, h, blocks, tag, copies):
-            y_sb = tile([P, len(blocks), BANK], F32, f"y_sb{h}{blocks[0]}", tag=tag)
-            for n, b in enumerate(blocks):
-                copies[n % len(copies)](y_sb[:, n, :], sums[b][:])
-                nc.sync.dma_start(out_0[b * P : (b + 1) * P, half(h)], y_sb[:, n, :])
-
-        zones_a = tile([P, PACK * BANK], F32, "zones_a", tag="spare")
-        for t in range(PACK):
-            fetch(zones_a, 0, t)
-        x_a = larger(zones_a, 0, "mid0")
-        zones_b = tile([P, PACK * BANK], F32, "zones_b", tag="spare")
-        fetch(zones_b, 1, 0)
-        close_sums(first_sums, 0, x_a)
-        hand_out(first_sums, 0, range(EARLY), "ten0", [nc.scalar.copy])
-        second_sums = open_sums(1, range(EARLY))
-        for t in range(1, PACK):
-            fetch(zones_b, 1, t)
+        def close_sum(plan, acc, y_sb, copy):
+            c0, width, blocks = plan
+            step = BANK if width == BANK else P
+            for place, b in enumerate(blocks):
+                for d in range(0, width, step):
+                    nc.tensor.matmul_mx(out=acc[:, place * width + d : place * width + d + step],
+                                        lhsT=w4_codes[:, 2 * b * P : 2 * (b + 1) * P].bitcast(FP4X4),
+                                        lhsT_scale=w4_sc[:, b * P : (b + 1) * P],
+                                        rhs=x_codes[:, c0 + d : c0 + d + step].bitcast(FP8X4),
+                                        rhs_scale=x_sc[:, c0 + d : c0 + d + step],
+                                        start=False, stop=(b == blocks[-1] and d + step == width))
+            used = len(blocks) * width
+            copy(y_sb[:, 0:used], acc[:, 0:used])
+            rows = out_0[blocks[0] * P : (blocks[-1] + 1) * P, c0 : c0 + width]
+            nc.sync.dma_start(rows.rearrange("(b p) j -> p b j", p=P),
+                              y_sb[:, 0:used].rearrange("p (b j) -> p b j", j=width))
 
         plane_codes = tile([P, T2], U32, "plane_codes")
         plane_sc = tile([P, T2], U8, "plane_sc")
         words_out = out_2[0].rearrange("p m t -> p (m t)").bitcast(I32)
-        for h in range(2):
+
+        def planes(h):
             cols = slice(h * T2 // 2, (h + 1) * T2 // 2)
             nc.vector.quantize_mx(out=plane_codes[:, cols].bitcast(FP8X4), scales=plane_sc[:, cols],
                                   in_=woven[h][:].bitcast(BF16))
             nc.sync.dma_start(words_out[:, cols], plane_codes[:, cols].bitcast(I32))
-            if h == 0:
-                hand_out(first_sums, 0, range(EARLY, BLOCKS), "mid1", [nc.scalar.copy])
-                second_sums = second_sums + open_sums(1, range(EARLY, BLOCKS))
-        for q in range(4):
-            nc.sync.dma_start(out_3[0, 4 * q : 4 * q + 4, :].bitcast(I32), plane_sc[32 * q : 32 * q + 4, :].bitcast(I32))
 
-        close_sums(second_sums, 1, larger(zones_b, 1, "mid2"))
-        hand_out(second_sums, 1, range(BLOCKS), "ten1", [nc.scalar.copy, nc.vector.tensor_copy])
+        last = len(PIECES) - 1
+        zones = tile([P, PACK * PIECES[0][1]], F32, "zones0", tag="spare")
+        for t in range(PACK):
+            fetch(zones, *PIECES[0], t)
+        for i, (c0, width) in enumerate(PIECES):
+            if i > 0:
+                planes(i - 1)
+            if i == last:
+                for q in range(4):
+                    nc.sync.dma_start(out_3[0, 4 * q : 4 * q + 4, :].bitcast(I32),
+                                      plane_sc[32 * q : 32 * q + 4, :].bitcast(I32))
+            x_bf = larger(zones, c0, width, f"mid{i}")
+            if i < last:
+                zones = tile([P, PACK * PIECES[i + 1][1]], F32, f"zones{i + 1}", tag="spare")
+                fetch(zones, *PIECES[i + 1], 0)
+            nc.vector.quantize_mx(out=x_codes[:, c0 : c0 + width].bitcast(FP8X4), scales=x_sc[:, c0 : c0 + width],
+                                  in_=x_bf[:])
+            y_sb = tile([P, len(plans[i]) * BANK], F32, f"y_sb{i}", tag=("ten0", "ten1", "wide2")[i])
+            for n, plan in enumerate(plans[i]):
+                copy = nc.vector.tensor_copy if i == last and n % 2 == 0 else nc.scalar.copy
+                close_sum(plan, sums[i][n], y_sb[:, n * BANK : (n + 1) * BANK], copy)
+            if i == 0:
+                sums.append([open_sum(plan, n) for n, plan in enumerate(plans[last])])
+            if i < last:
+                for t in range(1, PACK):
+                    fetch(zones, *PIECES[i + 1], t)

@@ -58,6 +58,10 @@ def tile_list_mirror_zone_page_kernel(tc, tab_words, tab_scales, offs, offs2, of
         one = tile([P, 1], F32, "one")
         nc.scalar.activation(one[:], one_in[:], ACT.Sqrt)
 
+        for q in range(4):
+            nc.gpsimd.dma_start(tab_sc[32 * q : 32 * q + 4 * PASSES, :].bitcast(I32),
+                                tab_scales[:, 4 * q : 4 * q + 4, :].bitcast(I32))
+
         wgs_sb = [tile([P, BANK], F32, f"wgs_sb{h}") for h in range(HALVES)]
         for h in range(HALVES):
             nc.sync.dma_start(wgs_sb[h][:], wgs[:, half(h)])
@@ -75,10 +79,6 @@ def tile_list_mirror_zone_page_kernel(tc, tab_words, tab_scales, offs, offs2, of
             words = tile([P, T], I32, f"tab{a}", tag=f"wide{a}")
             nc.sync.dma_start(words[:], tab_words[a].rearrange("p n t -> p (n t)").bitcast(I32))
             tab.append(words)
-            if a == 0:
-                for q in range(4):
-                    nc.sync.dma_start(tab_sc[32 * q : 32 * q + 4 * PASSES, :].bitcast(I32),
-                                      tab_scales[:, 4 * q : 4 * q + 4, :].bitcast(I32))
             raw = tile([P, PACK, H], F32, f"w1_raw{a}", tag=f"mid{a}")
             nc.sync.dma_start(raw[:], w1[a * 512 : (a + 1) * 512, :].rearrange("(p j) c -> p j c", j=PACK))
             w1_raw.append(raw)
@@ -161,23 +161,37 @@ def tile_list_mirror_zone_page_kernel(tc, tab_words, tab_scales, offs, offs2, of
 
         root = tile([P, PACK * S], F32, "root", tag="wide2")
         page_out = out_1.rearrange("(p t) c -> t p c", t=PACK)
-        for t in range(PACK):
-            for group in [group for group in groups if group[0] == t]:
-                c0, width = group[1:]
-                cols = slice(t * S + c0, t * S + c0 + width)
-                nc.scalar.activation(root[:, cols], strips[group][:, 0:width], ACT.Square)
-                nc.scalar.activation(root[:, cols], root[:, cols], ACT.Sqrt, bias=one[:])
-                if group == groups[0]:
-                    strips[groups[8]] = bank("strip8", 2)
-                    for a in range(PASSES):
-                        strip_pass(groups[8], a)
-                if t == 0:
-                    nc.vector.tensor_tensor(page[t][:].indirect(idx2[:, c0 // 16 : (c0 + width) // 16]), root[:, cols],
-                                            factor[:, cols], ALU.mult)
-            if t > 0:
+
+        def columns(group):
+            t, c0, width = group
+            return slice(t * S + c0, t * S + c0 + width)
+
+        def square(group):
+            nc.scalar.activation(root[:, columns(group)], strips[group][:, 0 : group[2]], ACT.Square)
+
+        def root_and_put(group):
+            t, c0, width = group
+            cols = columns(group)
+            nc.scalar.activation(root[:, cols], root[:, cols], ACT.Sqrt, bias=one[:])
+            if t == 0:
+                nc.vector.tensor_tensor(page[t][:].indirect(idx2[:, c0 // 16 : (c0 + width) // 16]), root[:, cols],
+                                        factor[:, cols], ALU.mult)
+            elif c0 + width == S:
                 whole = slice(t * S, (t + 1) * S)
                 nc.vector.tensor_tensor(page[t][:].indirect(idx2[:]), root[:, whole], factor[:, whole], ALU.mult)
-            nc.sync.dma_start(page_out[t], page[t][:])
+            if c0 + width == S:
+                nc.sync.dma_start(page_out[t], page[t][:])
+
+        square(groups[0])
+        root_and_put(groups[0])
+        strips[groups[8]] = bank("strip8", 2)
+        for a in range(PASSES):
+            strip_pass(groups[8], a)
+        square(groups[1])
+        for n in range(2, len(groups)):
+            square(groups[n])
+            root_and_put(groups[n - 1])
+        root_and_put(groups[-1])
 
         w3_bf = tile([P, PASSES * N * PACK], BF16, "w3_bf", tag="spare")
         w3_codes = tile([P, PASSES * N], U32, "w3_codes")

@@ -19,8 +19,12 @@ ALU = mybir.AluOpType
 
 P = 128
 PACK = 4
-PASSES = K // (P * PACK)
+K_PASS = P * PACK
+PASSES = K // K_PASS
+QUADS, QUAD = 4, 32
+LIST_COL = 16
 BANK = 512
+BANKS = 8
 HALVES = S // BANK
 BLOCKS = N // P
 LEAD = 256
@@ -41,11 +45,11 @@ def tile_list_mirror_zone_page_kernel(tc, tab_words, tab_scales, offs, offs2, of
         def bank(name, n):
             return psum.tile([P, BANK], F32, name=name, tag=f"bank{n}")
 
-        def half(h):
-            return slice(h * BANK, (h + 1) * BANK)
+        def entries(list_tile, c0, width):
+            return list_tile[:, c0 // LIST_COL : (c0 + width) // LIST_COL]
 
-        def list_half(h):
-            return slice(h * BANK // 16, (h + 1) * BANK // 16)
+        def pass_rows(weight, a):
+            return weight[a * K_PASS : (a + 1) * K_PASS, :].rearrange("(p j) c -> p j c", j=PACK)
 
         ident = tile([P, P], F32, "ident")
         make_identity(nc, ident[:])
@@ -58,20 +62,20 @@ def tile_list_mirror_zone_page_kernel(tc, tab_words, tab_scales, offs, offs2, of
         one = tile([P, 1], F32, "one")
         nc.scalar.activation(one[:], one_in[:], ACT.Sqrt)
 
-        for q in range(4):
-            nc.gpsimd.dma_start(tab_sc[32 * q : 32 * q + 4 * PASSES, :].bitcast(I32),
+        for q in range(QUADS):
+            nc.gpsimd.dma_start(tab_sc[QUAD * q : QUAD * q + 4 * PASSES, :].bitcast(I32),
                                 tab_scales[:, 4 * q : 4 * q + 4, :].bitcast(I32))
 
         wgs_sb = [tile([P, BANK], F32, f"wgs_sb{h}") for h in range(HALVES)]
         for h in range(HALVES):
-            nc.sync.dma_start(wgs_sb[h][:], wgs[:, half(h)])
-        idx = lists.tile([P, S // 16], U16, name="idx")
+            nc.sync.dma_start(wgs_sb[h][:], wgs[:, h * BANK : (h + 1) * BANK])
+        idx = lists.tile([P, S // LIST_COL], U16, name="idx")
         nc.sync.dma_start(idx[:], offs)
         gain_sb = tile([P, PACK], F32, "gain_sb")
         nc.sync.dma_start(gain_sb[:], gain.rearrange("(p t) -> p t", t=PACK))
-        idx2 = lists.tile([P, S // 16], U16, name="idx2")
+        idx2 = lists.tile([P, S // LIST_COL], U16, name="idx2")
         nc.sync.dma_start(idx2[:], offs2)
-        idx3 = lists.tile([P, S // 16], U16, name="idx3")
+        idx3 = lists.tile([P, S // LIST_COL], U16, name="idx3")
         nc.sync.dma_start(idx3[:], offs3)
         tab = []
         w1_raw = []
@@ -80,86 +84,90 @@ def tile_list_mirror_zone_page_kernel(tc, tab_words, tab_scales, offs, offs2, of
             nc.sync.dma_start(words[:], tab_words[a].rearrange("p n t -> p (n t)").bitcast(I32))
             tab.append(words)
             raw = tile([P, PACK, H], F32, f"w1_raw{a}", tag=f"mid{a}")
-            nc.sync.dma_start(raw[:], w1[a * 512 : (a + 1) * 512, :].rearrange("(p j) c -> p j c", j=PACK))
+            nc.sync.dma_start(raw[:], pass_rows(w1, a))
             w1_raw.append(raw)
         page_rows = page0.rearrange("(p t) c -> t p c", t=PACK)
         page = [tile([P, T2], F32, f"page{t}") for t in range(PACK)]
         w3_raw = [tile([P, PACK, N], F32, f"w3_raw{a}", tag=f"ten{a}") for a in range(PASSES - 1)]
 
         wgs_t = tile([P, PACK * S], F32, "wgs_t", tag="spare")
-        wgs_t5 = wgs_t[:].rearrange("j (b t r q) -> j b t r q", t=PACK, r=4, q=32)
+        wgs_t5 = wgs_t[:].rearrange("j (b t r q) -> j b t r q", t=PACK, r=QUADS, q=QUAD)
+        per_bank = BANK // P
         for h in range(HALVES):
             turned = bank("turned", h)
-            for b in range(4):
+            for b in range(per_bank):
                 nc.tensor.transpose(turned[:, b * P : (b + 1) * P], wgs_sb[h][:, b * P : (b + 1) * P], ident[:])
-            src = turned[:].rearrange("j (b q t) -> j b t q", t=PACK, q=32).unsqueeze(3).to_broadcast([P, 4, PACK, 4, 32])
-            if h == 0:
-                nc.scalar.copy(wgs_t5[:, 4 * h : 4 * h + 4], src)
-            else:
-                nc.vector.tensor_copy(wgs_t5[:, 4 * h : 4 * h + 4], src)
+            src = turned[:].rearrange("j (b q t) -> j b t q", t=PACK, q=QUAD).unsqueeze(3)
+            copy = nc.scalar.copy if h == 0 else nc.vector.tensor_copy
+            copy(wgs_t5[:, per_bank * h : per_bank * (h + 1)], src.to_broadcast([P, per_bank, PACK, QUADS, QUAD]))
         factor = tile([P, PACK * S], F32, "factor")
         for t in range(PACK):
             for h in range(HALVES):
-                back = bank("back", (2 + HALVES * t + h) % 8)
-                for b in range(4):
-                    start = ((4 * h + b) * PACK + t) * P
+                back = bank("back", (HALVES + HALVES * t + h) % BANKS)
+                for b in range(per_bank):
+                    start = ((per_bank * h + b) * PACK + t) * P
                     nc.tensor.transpose(back[:, b * P : (b + 1) * P], wgs_t[:, start : start + P], ident[:])
                 nc.scalar.activation(factor[:, t * S + h * BANK : t * S + (h + 1) * BANK], back[:], ACT.Copy,
                                      scale=gain_sb[:, t : t + 1])
 
-        v = []
+        v = {}
+
+        def pick(a, h, tag=None):
+            v[a, h] = tile([P, BANK], U32, f"v{a}{h}", tag=tag)
+            nc.vector.tensor_copy(v[a, h][:], tab[a][:].bitcast(U32).indirect(entries(idx, h * BANK, BANK)))
+
+        def picked(a, c0, width):
+            return v[a, c0 // BANK][:, c0 % BANK : c0 % BANK + width].bitcast(FP8X4)
+
         v_sc = tile([P, S], U8, "v_sc")
-        groups = [(0, 0, LEAD), (0, LEAD, BANK - LEAD)] + [(t, h * BANK, BANK) for t in range(PACK) for h in range(HALVES)][1:]
-        strips = {group: bank(f"strip{n}", (2 + n) % 8) for n, group in enumerate(groups[:8])}
+        groups = [(0, 0, LEAD), (0, LEAD, BANK - LEAD)]
+        groups = groups + [(t, h * BANK, BANK) for t in range(PACK) for h in range(HALVES)][1:]
+        strips = {group: bank(f"strip{n}", (HALVES + n) % BANKS) for n, group in enumerate(groups[:BANKS])}
         w1_q = {}
 
         def strip_pass(group, a):
             t, c0, width = group
             codes, scales = w1_q[a, t // 2]
             cols = slice(t % 2 * P, (t % 2 + 1) * P)
-            nc.tensor.matmul_mx(out=strips[group][:, 0:width], lhsT=codes[:, cols].bitcast(FP8X4), lhsT_scale=scales[:, cols],
-                                rhs=v[a][:, c0 : c0 + width].bitcast(FP8X4), rhs_scale=v_sc[4 * a : P, c0 : c0 + width],
-                                start=(a == 0), stop=(a == PASSES - 1))
+            nc.tensor.matmul_mx(out=strips[group][:, 0:width], lhsT=codes[:, cols].bitcast(FP8X4),
+                                lhsT_scale=scales[:, cols], rhs=picked(a, c0, width),
+                                rhs_scale=v_sc[4 * a : P, c0 : c0 + width], start=(a == 0), stop=(a == PASSES - 1))
 
         for a in range(PASSES):
-            picked = tile([P, S], U32, f"v{a}")
-            nc.vector.tensor_copy(picked[:], tab[a][:].bitcast(U32).indirect(idx[:]))
-            v.append(picked)
+            pick(a, 0)
+            if a < PASSES - 1:
+                pick(a, 1)
             if a == 0:
                 nc.vector.tensor_copy(v_sc[:], tab_sc[:].indirect(idx[:]))
             for u in range(2):
                 grouped = tile([P, 2 * P * PACK], BF16, f"w1_bf{a}{u}")
-                dst = grouped[:].rearrange("p (e m j) -> p m j e", e=2, j=PACK)
-                src = w1_raw[a][:].rearrange("p j (m u e) -> p u m j e", u=2, e=2)[:, u]
-                if u == 0:
-                    nc.vector.tensor_copy(dst, src)
-                else:
-                    nc.scalar.copy(dst, src)
+                copy = nc.vector.tensor_copy if u == 0 else nc.scalar.copy
+                copy(grouped[:].rearrange("p (e m j) -> p m j e", e=2, j=PACK),
+                     w1_raw[a][:].rearrange("p j (m u e) -> p u m j e", u=2, e=2)[:, u])
                 codes = tile([P, 2 * P], U32, f"w1_codes{a}{u}")
                 scales = tile([P, 2 * P], U8, f"w1_sc{a}{u}")
                 nc.vector.quantize_mx(out=codes[:].bitcast(FP8X4), scales=scales[:], in_=grouped[:])
                 w1_q[a, u] = (codes, scales)
-                for group in groups[:8]:
+                if a == PASSES - 1 and u == 0:
+                    pick(a, 1, f"w1_bf{a}{u}")
+                for group in groups[:BANKS]:
                     if group[0] // 2 == u:
                         strip_pass(group, a)
 
         w3_raw.append(tile([P, PACK, N], F32, "w3_raw2", tag="wide1"))
-        target_sb = tile([P, PACK, S], F32, "target_sb", tag="wide0")
-
-        def load_w3(a):
-            nc.sync.dma_start(w3_raw[a][:], w3[a * 512 : (a + 1) * 512, :].rearrange("(p j) c -> p j c", j=PACK))
-
+        target_sb = tile([P, PACK, S], F32, "target_sb", tag="wide2")
         for a in range(PASSES):
             nc.sync.dma_start(page[a][:], page_rows[a])
-            load_w3(a)
-        nc.sync.dma_start(page[PASSES][:], page_rows[PASSES])
+            nc.sync.dma_start(w3_raw[a][:], pass_rows(w3, a))
+        nc.sync.dma_start(page[PACK - 1][:], page_rows[PACK - 1])
         w4_codes = tile([P, 2 * N], U8, "w4_codes")
         nc.sync.dma_start(w4_codes[:].bitcast(I32), w4_words[0].bitcast(I32))
-        for q in range(4):
-            nc.sync.dma_start(w4_sc[32 * q : 32 * q + 4, :].bitcast(I32), w4_scales[0, 4 * q : 4 * q + 4, :].bitcast(I32))
+        for q in range(QUADS):
+            nc.sync.dma_start(w4_sc[QUAD * q : QUAD * q + 4, :].bitcast(I32),
+                              w4_scales[0, 4 * q : 4 * q + 4, :].bitcast(I32))
         nc.sync.dma_start(target_sb[:], target.rearrange("(p t) j -> p t j", t=PACK))
 
-        root = tile([P, PACK * S], F32, "root", tag="wide2")
+        root = tile([P, PACK * S], F32, "root", tag="wide0")
         page_out = out_1.rearrange("(p t) c -> t p c", t=PACK)
 
         def columns(group):
@@ -174,7 +182,7 @@ def tile_list_mirror_zone_page_kernel(tc, tab_words, tab_scales, offs, offs2, of
             cols = columns(group)
             nc.scalar.activation(root[:, cols], root[:, cols], ACT.Sqrt, bias=one[:])
             if t == 0:
-                nc.vector.tensor_tensor(page[t][:].indirect(idx2[:, c0 // 16 : (c0 + width) // 16]), root[:, cols],
+                nc.vector.tensor_tensor(page[t][:].indirect(entries(idx2, c0, width)), root[:, cols],
                                         factor[:, cols], ALU.mult)
             elif c0 + width == S:
                 whole = slice(t * S, (t + 1) * S)
@@ -184,9 +192,9 @@ def tile_list_mirror_zone_page_kernel(tc, tab_words, tab_scales, offs, offs2, of
 
         square(groups[0])
         root_and_put(groups[0])
-        strips[groups[8]] = bank("strip8", 2)
+        strips[groups[BANKS]] = bank("strip_last", HALVES)
         for a in range(PASSES):
-            strip_pass(groups[8], a)
+            strip_pass(groups[BANKS], a)
         square(groups[1])
         for n in range(2, len(groups)):
             square(groups[n])
@@ -199,13 +207,13 @@ def tile_list_mirror_zone_page_kernel(tc, tab_words, tab_scales, offs, offs2, of
         for a in range(PASSES):
             dst = w3_bf[:, a * N * PACK : (a + 1) * N * PACK].rearrange("p (c i j) -> p c j i", i=2, j=PACK)
             nc.scalar.copy(dst, w3_raw[a][:].rearrange("p j (c i) -> p c j i", i=2))
-            for c0, c1 in ((a * N, a * N + 512), (a * N + 512, (a + 1) * N)):
+            for c0, c1 in ((a * N, a * N + BANK), (a * N + BANK, (a + 1) * N)):
                 nc.vector.quantize_mx(out=w3_codes[:, c0:c1].bitcast(FP8X4), scales=w3_sc[:, c0:c1],
                                       in_=w3_bf[:, c0 * PACK : c1 * PACK])
 
-        def bank_plan(c0, width):
-            per_bank = BANK // width
-            return [(c0, width, list(range(b, min(b + per_bank, BLOCKS)))) for b in range(0, BLOCKS, per_bank)]
+        def bank_plans(c0, width):
+            side_by_side = BANK // width
+            return [(c0, width, list(range(b, min(b + side_by_side, BLOCKS)))) for b in range(0, BLOCKS, side_by_side)]
 
         def open_sum(plan, n):
             c0, width, blocks = plan
@@ -215,12 +223,11 @@ def tile_list_mirror_zone_page_kernel(tc, tab_words, tab_scales, offs, offs2, of
                     cols = slice(a * N + b * P, a * N + (b + 1) * P)
                     nc.tensor.matmul_mx(out=acc[:, place * width : (place + 1) * width],
                                         lhsT=w3_codes[:, cols].bitcast(FP8X4), lhsT_scale=w3_sc[:, cols],
-                                        rhs=v[a][:, c0 : c0 + width].bitcast(FP8X4),
-                                        rhs_scale=v_sc[4 * a : P, c0 : c0 + width],
+                                        rhs=picked(a, c0, width), rhs_scale=v_sc[4 * a : P, c0 : c0 + width],
                                         start=(place == 0 and a == 0), stop=False)
             return acc
 
-        plans = [bank_plan(c0, width) for c0, width in PIECES]
+        plans = [bank_plans(c0, width) for c0, width in PIECES]
         sums = [[open_sum(plan, n) for n, plan in enumerate(plans[0])]]
         sums.append([open_sum(plan, len(plans[0]) + n) for n, plan in enumerate(plans[1])])
 
@@ -239,17 +246,20 @@ def tile_list_mirror_zone_page_kernel(tc, tab_words, tab_scales, offs, offs2, of
         x_codes = tile([P, S], U32, "x_codes")
         x_sc = tile([P, S], U8, "x_sc")
 
-        def fetch(zones, c0, width, t):
-            nc.vector.tensor_copy(zones[:, t * width : (t + 1) * width],
-                                  page[t][:].indirect(idx3[:, c0 // 16 : (c0 + width) // 16]))
+        def zone_tile(i):
+            return tile([P, PACK * PIECES[i][1]], F32, f"zones{i}", tag="spare")
 
-        def larger(zones, c0, width, tag):
-            x_bf = tile([P, width * PACK], BF16, f"x_bf{c0}", tag=tag)
-            nc.vector.tensor_tensor(
-                x_bf[:].rearrange("p (c i t) -> p c t i", i=2, t=PACK),
-                zones[:].rearrange("p (t c i) -> p c t i", i=2, t=PACK),
-                target_sb[:, :, c0 : c0 + width].rearrange("p t (c i) -> p c t i", i=2),
-                ALU.max)
+        def fetch(zones, i, t):
+            c0, width = PIECES[i]
+            nc.vector.tensor_copy(zones[:, t * width : (t + 1) * width], page[t][:].indirect(entries(idx3, c0, width)))
+
+        def larger(zones, i):
+            c0, width = PIECES[i]
+            x_bf = tile([P, width * PACK], BF16, f"x_bf{c0}", tag=f"mid{i}")
+            nc.vector.tensor_tensor(x_bf[:].rearrange("p (c i t) -> p c t i", i=2, t=PACK),
+                                    zones[:].rearrange("p (t c i) -> p c t i", i=2, t=PACK),
+                                    target_sb[:, :, c0 : c0 + width].rearrange("p t (c i) -> p c t i", i=2),
+                                    ALU.max)
             return x_bf
 
         def close_sum(plan, acc, y_sb, copy):
@@ -269,39 +279,41 @@ def tile_list_mirror_zone_page_kernel(tc, tab_words, tab_scales, offs, offs2, of
             nc.sync.dma_start(rows.rearrange("(b p) j -> p b j", p=P),
                               y_sb[:, 0:used].rearrange("p (b j) -> p b j", j=width))
 
-        plane_codes = tile([P, T2], U32, "plane_codes")
-        plane_sc = tile([P, T2], U8, "plane_sc")
+        page_codes = tile([P, T2], U32, "page_codes")
+        page_sc = tile([P, T2], U8, "page_sc")
         words_out = out_2[0].rearrange("p m t -> p (m t)").bitcast(I32)
 
-        def planes(h):
+        def quantise_page(h):
             cols = slice(h * T2 // 2, (h + 1) * T2 // 2)
-            nc.vector.quantize_mx(out=plane_codes[:, cols].bitcast(FP8X4), scales=plane_sc[:, cols],
+            nc.vector.quantize_mx(out=page_codes[:, cols].bitcast(FP8X4), scales=page_sc[:, cols],
                                   in_=woven[h][:].bitcast(BF16))
-            nc.sync.dma_start(words_out[:, cols], plane_codes[:, cols].bitcast(I32))
+            nc.sync.dma_start(words_out[:, cols], page_codes[:, cols].bitcast(I32))
 
         last = len(PIECES) - 1
-        zones = tile([P, PACK * PIECES[0][1]], F32, "zones0", tag="spare")
+        zones = zone_tile(0)
         for t in range(PACK):
-            fetch(zones, *PIECES[0], t)
+            fetch(zones, 0, t)
         for i, (c0, width) in enumerate(PIECES):
             if i > 0:
-                planes(i - 1)
+                quantise_page(i - 1)
             if i == last:
-                for q in range(4):
+                for q in range(QUADS):
                     nc.sync.dma_start(out_3[0, 4 * q : 4 * q + 4, :].bitcast(I32),
-                                      plane_sc[32 * q : 32 * q + 4, :].bitcast(I32))
-            x_bf = larger(zones, c0, width, f"mid{i}")
+                                      page_sc[QUAD * q : QUAD * q + 4, :].bitcast(I32))
+            x_bf = larger(zones, i)
             if i < last:
-                zones = tile([P, PACK * PIECES[i + 1][1]], F32, f"zones{i + 1}", tag="spare")
-                fetch(zones, *PIECES[i + 1], 0)
+                zones = zone_tile(i + 1)
+                fetch(zones, i + 1, 0)
             nc.vector.quantize_mx(out=x_codes[:, c0 : c0 + width].bitcast(FP8X4), scales=x_sc[:, c0 : c0 + width],
                                   in_=x_bf[:])
-            y_sb = tile([P, len(plans[i]) * BANK], F32, f"y_sb{i}", tag=("ten0", "ten1", "wide2")[i])
+            y_sb = tile([P, len(plans[i]) * BANK], F32, f"y_sb{i}", tag=("ten0", "ten1", "wide0")[i])
             for n, plan in enumerate(plans[i]):
                 copy = nc.vector.tensor_copy if i == last and n % 2 == 0 else nc.scalar.copy
                 close_sum(plan, sums[i][n], y_sb[:, n * BANK : (n + 1) * BANK], copy)
             if i == 0:
-                sums.append([open_sum(plan, n) for n, plan in enumerate(plans[last])])
+                sums.append([open_sum(plans[last][0], 0)])
+            if i == 1:
+                sums[last].extend(open_sum(plan, len(plans[0]) + n) for n, plan in enumerate(plans[last][1:]))
             if i < last:
                 for t in range(1, PACK):
-                    fetch(zones, *PIECES[i + 1], t)
+                    fetch(zones, i + 1, t)

from contextlib import ExitStack

import concourse.mybir as mybir
from concourse.masks import make_identity

K, T, S, H, T2, N = 1536, 4096, 1024, 512, 2048, 640
FLOPS = 2 * K * H * S + 2 * H * N * S + 2 * K * N * S

F32 = mybir.dt.float32
BF16 = mybir.dt.bfloat16
I32 = mybir.dt.int32
U32 = mybir.dt.uint32
U16 = mybir.dt.uint16
U8 = mybir.dt.uint8
FP8X4 = mybir.dt.float8_e4m3fn_x4
FP4X4 = mybir.dt.float4_e2m1fn_x4
ACT = mybir.ActivationFunctionType
ALU = mybir.AluOpType

P = 128
PACK = 4
K_PASS = P * PACK
PASSES = K // K_PASS
QUADS, QUAD = 4, 32
LIST_COL = 16
BANK = 512
BANKS = 8
HALVES = S // BANK
BLOCKS = N // P
LEAD = 256
PIECES = ((0, 512), (512, 256), (768, 256))


def tile_list_mirror_zone_page_kernel(tc, tab_words, tab_scales, offs, offs2, offs3, w1, gain, wgs, page0,
                                               target, w4_words, w4_scales, w3, out_0, out_1, out_2, out_3):
    nc = tc.nc
    with ExitStack() as ctx:
        lists = ctx.enter_context(tc.tile_pool(name="lists", bufs=1))
        sb = ctx.enter_context(tc.tile_pool(name="sb", bufs=1))
        psum = ctx.enter_context(tc.psum_pool(name="psum", bufs=1))

        def tile(shape, dtype, name, tag=None):
            return sb.tile(shape, dtype, name=name, tag=tag or name, align_bytes=64)

        def bank(name, n):
            return psum.tile([P, BANK], F32, name=name, tag=f"bank{n}")

        def entries(list_tile, c0, width):
            return list_tile[:, c0 // LIST_COL : (c0 + width) // LIST_COL]

        def pass_rows(weight, a):
            return weight[a * K_PASS : (a + 1) * K_PASS, :].rearrange("(p j) c -> p j c", j=PACK)

        ident = tile([P, P], F32, "ident")
        make_identity(nc, ident[:])
        tab_sc = tile([P, T], U8, "tab_sc")
        nc.vector.memset(tab_sc[:].bitcast(I32), 0)
        w4_sc = tile([P, N], U8, "w4_sc")
        nc.vector.memset(w4_sc[:].bitcast(I32), 0)
        one_in = tile([P, 1], F32, "one_in")
        nc.vector.memset(one_in[:], 1.0)
        one = tile([P, 1], F32, "one")
        nc.scalar.activation(one[:], one_in[:], ACT.Sqrt)

        for q in range(QUADS):
            nc.gpsimd.dma_start(tab_sc[QUAD * q : QUAD * q + 4 * PASSES, :].bitcast(I32),
                                tab_scales[:, 4 * q : 4 * q + 4, :].bitcast(I32))

        wgs_sb = [tile([P, BANK], F32, f"wgs_sb{h}") for h in range(HALVES)]
        for h in range(HALVES):
            nc.sync.dma_start(wgs_sb[h][:], wgs[:, h * BANK : (h + 1) * BANK])
        idx = lists.tile([P, S // LIST_COL], U16, name="idx")
        nc.sync.dma_start(idx[:], offs)
        gain_sb = tile([P, PACK], F32, "gain_sb")
        nc.sync.dma_start(gain_sb[:], gain.rearrange("(p t) -> p t", t=PACK))
        idx2 = lists.tile([P, S // LIST_COL], U16, name="idx2")
        nc.sync.dma_start(idx2[:], offs2)
        idx3 = lists.tile([P, S // LIST_COL], U16, name="idx3")
        nc.sync.dma_start(idx3[:], offs3)
        tab = []
        w1_raw = []
        for a in range(PASSES):
            words = tile([P, T], I32, f"tab{a}", tag=f"wide{a}")
            nc.sync.dma_start(words[:], tab_words[a].rearrange("p n t -> p (n t)").bitcast(I32))
            tab.append(words)
            raw = tile([P, PACK, H], F32, f"w1_raw{a}", tag=f"mid{a}")
            nc.sync.dma_start(raw[:], pass_rows(w1, a))
            w1_raw.append(raw)
        page_rows = page0.rearrange("(p t) c -> t p c", t=PACK)
        page = [tile([P, T2], F32, f"page{t}") for t in range(PACK)]
        w3_raw = [tile([P, PACK, N], F32, f"w3_raw{a}", tag=f"ten{a}") for a in range(PASSES - 1)]

        wgs_t = tile([P, PACK * S], F32, "wgs_t", tag="spare")
        wgs_t5 = wgs_t[:].rearrange("j (b t r q) -> j b t r q", t=PACK, r=QUADS, q=QUAD)
        per_bank = BANK // P
        for h in range(HALVES):
            turned = bank("turned", h)
            for b in range(per_bank):
                nc.tensor.transpose(turned[:, b * P : (b + 1) * P], wgs_sb[h][:, b * P : (b + 1) * P], ident[:])
            src = turned[:].rearrange("j (b q t) -> j b t q", t=PACK, q=QUAD).unsqueeze(3)
            copy = nc.scalar.copy if h == 0 else nc.vector.tensor_copy
            copy(wgs_t5[:, per_bank * h : per_bank * (h + 1)], src.to_broadcast([P, per_bank, PACK, QUADS, QUAD]))
        factor = tile([P, PACK * S], F32, "factor")
        for t in range(PACK):
            for h in range(HALVES):
                back = bank("back", (HALVES + HALVES * t + h) % BANKS)
                for b in range(per_bank):
                    start = ((per_bank * h + b) * PACK + t) * P
                    nc.tensor.transpose(back[:, b * P : (b + 1) * P], wgs_t[:, start : start + P], ident[:])
                nc.scalar.activation(factor[:, t * S + h * BANK : t * S + (h + 1) * BANK], back[:], ACT.Copy,
                                     scale=gain_sb[:, t : t + 1])

        v = {}

        def pick(a, h, tag=None):
            v[a, h] = tile([P, BANK], U32, f"v{a}{h}", tag=tag)
            nc.vector.tensor_copy(v[a, h][:], tab[a][:].bitcast(U32).indirect(entries(idx, h * BANK, BANK)))

        def picked(a, c0, width):
            return v[a, c0 // BANK][:, c0 % BANK : c0 % BANK + width].bitcast(FP8X4)

        v_sc = tile([P, S], U8, "v_sc")
        groups = [(0, 0, LEAD), (0, LEAD, BANK - LEAD)]
        groups = groups + [(t, h * BANK, BANK) for t in range(PACK) for h in range(HALVES)][1:]
        strips = {group: bank(f"strip{n}", (HALVES + n) % BANKS) for n, group in enumerate(groups[:BANKS])}
        w1_q = {}

        def strip_pass(group, a):
            t, c0, width = group
            codes, scales = w1_q[a, t // 2]
            cols = slice(t % 2 * P, (t % 2 + 1) * P)
            nc.tensor.matmul_mx(out=strips[group][:, 0:width], lhsT=codes[:, cols].bitcast(FP8X4),
                                lhsT_scale=scales[:, cols], rhs=picked(a, c0, width),
                                rhs_scale=v_sc[4 * a : P, c0 : c0 + width], start=(a == 0), stop=(a == PASSES - 1))

        for a in range(PASSES):
            pick(a, 0)
            if a < PASSES - 1:
                pick(a, 1)
            if a == 0:
                nc.vector.tensor_copy(v_sc[:], tab_sc[:].indirect(idx[:]))
            for u in range(2):
                grouped = tile([P, 2 * P * PACK], BF16, f"w1_bf{a}{u}")
                copy = nc.vector.tensor_copy if u == 0 else nc.scalar.copy
                copy(grouped[:].rearrange("p (e m j) -> p m j e", e=2, j=PACK),
                     w1_raw[a][:].rearrange("p j (m u e) -> p u m j e", u=2, e=2)[:, u])
                codes = tile([P, 2 * P], U32, f"w1_codes{a}{u}")
                scales = tile([P, 2 * P], U8, f"w1_sc{a}{u}")
                nc.vector.quantize_mx(out=codes[:].bitcast(FP8X4), scales=scales[:], in_=grouped[:])
                w1_q[a, u] = (codes, scales)
                if a == PASSES - 1 and u == 0:
                    pick(a, 1, f"w1_bf{a}{u}")
                for group in groups[:BANKS]:
                    if group[0] // 2 == u:
                        strip_pass(group, a)

        w3_raw.append(tile([P, PACK, N], F32, "w3_raw2", tag="wide1"))
        target_sb = tile([P, PACK, S], F32, "target_sb", tag="wide2")
        for a in range(PASSES):
            nc.sync.dma_start(page[a][:], page_rows[a])
            nc.sync.dma_start(w3_raw[a][:], pass_rows(w3, a))
        nc.sync.dma_start(page[PACK - 1][:], page_rows[PACK - 1])
        w4_codes = tile([P, 2 * N], U8, "w4_codes")
        nc.sync.dma_start(w4_codes[:].bitcast(I32), w4_words[0].bitcast(I32))
        for q in range(QUADS):
            nc.sync.dma_start(w4_sc[QUAD * q : QUAD * q + 4, :].bitcast(I32),
                              w4_scales[0, 4 * q : 4 * q + 4, :].bitcast(I32))
        nc.sync.dma_start(target_sb[:], target.rearrange("(p t) j -> p t j", t=PACK))

        root = tile([P, PACK * S], F32, "root", tag="wide0")
        page_out = out_1.rearrange("(p t) c -> t p c", t=PACK)

        def columns(group):
            t, c0, width = group
            return slice(t * S + c0, t * S + c0 + width)

        def square(group):
            nc.scalar.activation(root[:, columns(group)], strips[group][:, 0 : group[2]], ACT.Square)

        def root_and_put(group):
            t, c0, width = group
            cols = columns(group)
            nc.scalar.activation(root[:, cols], root[:, cols], ACT.Sqrt, bias=one[:])
            if t == 0:
                nc.vector.tensor_tensor(page[t][:].indirect(entries(idx2, c0, width)), root[:, cols],
                                        factor[:, cols], ALU.mult)
            elif c0 + width == S:
                whole = slice(t * S, (t + 1) * S)
                nc.vector.tensor_tensor(page[t][:].indirect(idx2[:]), root[:, whole], factor[:, whole], ALU.mult)
            if c0 + width == S:
                nc.sync.dma_start(page_out[t], page[t][:])

        square(groups[0])
        root_and_put(groups[0])
        strips[groups[BANKS]] = bank("strip_last", HALVES)
        for a in range(PASSES):
            strip_pass(groups[BANKS], a)
        square(groups[1])
        for n in range(2, len(groups)):
            square(groups[n])
            root_and_put(groups[n - 1])
        root_and_put(groups[-1])

        w3_bf = tile([P, PASSES * N * PACK], BF16, "w3_bf", tag="spare")
        w3_codes = tile([P, PASSES * N], U32, "w3_codes")
        w3_sc = tile([P, PASSES * N], U8, "w3_sc")
        for a in range(PASSES):
            dst = w3_bf[:, a * N * PACK : (a + 1) * N * PACK].rearrange("p (c i j) -> p c j i", i=2, j=PACK)
            nc.scalar.copy(dst, w3_raw[a][:].rearrange("p j (c i) -> p c j i", i=2))
            for c0, c1 in ((a * N, a * N + BANK), (a * N + BANK, (a + 1) * N)):
                nc.vector.quantize_mx(out=w3_codes[:, c0:c1].bitcast(FP8X4), scales=w3_sc[:, c0:c1],
                                      in_=w3_bf[:, c0 * PACK : c1 * PACK])

        def bank_plans(c0, width):
            side_by_side = BANK // width
            return [(c0, width, list(range(b, min(b + side_by_side, BLOCKS)))) for b in range(0, BLOCKS, side_by_side)]

        def open_sum(plan, n):
            c0, width, blocks = plan
            acc = bank(f"y{c0}_{blocks[0]}", n)
            for place, b in enumerate(blocks):
                for a in range(PASSES):
                    cols = slice(a * N + b * P, a * N + (b + 1) * P)
                    nc.tensor.matmul_mx(out=acc[:, place * width : (place + 1) * width],
                                        lhsT=w3_codes[:, cols].bitcast(FP8X4), lhsT_scale=w3_sc[:, cols],
                                        rhs=picked(a, c0, width), rhs_scale=v_sc[4 * a : P, c0 : c0 + width],
                                        start=(place == 0 and a == 0), stop=False)
            return acc

        plans = [bank_plans(c0, width) for c0, width in PIECES]
        sums = [[open_sum(plan, n) for n, plan in enumerate(plans[0])]]
        sums.append([open_sum(plan, len(plans[0]) + n) for n, plan in enumerate(plans[1])])

        pairs = tile([P, PACK * T2], BF16, "pairs", tag="wide1")
        pairs4 = pairs[:].rearrange("p (u c e) -> p u e c", u=2, e=2)
        for t in range(PACK):
            nc.scalar.copy(pairs4[:, t // 2, t % 2], page[t][:])
        pair_words = pairs[:].bitcast(F32).rearrange("p (u c i) -> p c u i", u=2, i=2)
        woven = []
        for h in range(2):
            part = tile([P, T2], F32, f"woven{h}", tag=f"mid{h + 1}")
            nc.scalar.copy(part[:].rearrange("p (c i u) -> p c u i", u=2, i=2),
                           pair_words[:, h * T2 // 4 : (h + 1) * T2 // 4])
            woven.append(part)

        x_codes = tile([P, S], U32, "x_codes")
        x_sc = tile([P, S], U8, "x_sc")

        def zone_tile(i):
            return tile([P, PACK * PIECES[i][1]], F32, f"zones{i}", tag="spare")

        def fetch(zones, i, t):
            c0, width = PIECES[i]
            nc.vector.tensor_copy(zones[:, t * width : (t + 1) * width], page[t][:].indirect(entries(idx3, c0, width)))

        def larger(zones, i):
            c0, width = PIECES[i]
            x_bf = tile([P, width * PACK], BF16, f"x_bf{c0}", tag=f"mid{i}")
            nc.vector.tensor_tensor(x_bf[:].rearrange("p (c i t) -> p c t i", i=2, t=PACK),
                                    zones[:].rearrange("p (t c i) -> p c t i", i=2, t=PACK),
                                    target_sb[:, :, c0 : c0 + width].rearrange("p t (c i) -> p c t i", i=2),
                                    ALU.max)
            return x_bf

        def close_sum(plan, acc, y_sb, copy):
            c0, width, blocks = plan
            step = BANK if width == BANK else P
            for place, b in enumerate(blocks):
                for d in range(0, width, step):
                    nc.tensor.matmul_mx(out=acc[:, place * width + d : place * width + d + step],
                                        lhsT=w4_codes[:, 2 * b * P : 2 * (b + 1) * P].bitcast(FP4X4),
                                        lhsT_scale=w4_sc[:, b * P : (b + 1) * P],
                                        rhs=x_codes[:, c0 + d : c0 + d + step].bitcast(FP8X4),
                                        rhs_scale=x_sc[:, c0 + d : c0 + d + step],
                                        start=False, stop=(b == blocks[-1] and d + step == width))
            used = len(blocks) * width
            copy(y_sb[:, 0:used], acc[:, 0:used])
            rows = out_0[blocks[0] * P : (blocks[-1] + 1) * P, c0 : c0 + width]
            nc.sync.dma_start(rows.rearrange("(b p) j -> p b j", p=P),
                              y_sb[:, 0:used].rearrange("p (b j) -> p b j", j=width))

        page_codes = tile([P, T2], U32, "page_codes")
        page_sc = tile([P, T2], U8, "page_sc")
        words_out = out_2[0].rearrange("p m t -> p (m t)").bitcast(I32)

        def quantise_page(h):
            cols = slice(h * T2 // 2, (h + 1) * T2 // 2)
            nc.vector.quantize_mx(out=page_codes[:, cols].bitcast(FP8X4), scales=page_sc[:, cols],
                                  in_=woven[h][:].bitcast(BF16))
            nc.sync.dma_start(words_out[:, cols], page_codes[:, cols].bitcast(I32))

        last = len(PIECES) - 1
        zones = zone_tile(0)
        for t in range(PACK):
            fetch(zones, 0, t)
        for i, (c0, width) in enumerate(PIECES):
            if i > 0:
                quantise_page(i - 1)
            if i == last:
                for q in range(QUADS):
                    nc.sync.dma_start(out_3[0, 4 * q : 4 * q + 4, :].bitcast(I32),
                                      page_sc[QUAD * q : QUAD * q + 4, :].bitcast(I32))
            x_bf = larger(zones, i)
            if i < last:
                zones = zone_tile(i + 1)
                fetch(zones, i + 1, 0)
            nc.vector.quantize_mx(out=x_codes[:, c0 : c0 + width].bitcast(FP8X4), scales=x_sc[:, c0 : c0 + width],
                                  in_=x_bf[:])
            y_sb = tile([P, len(plans[i]) * BANK], F32, f"y_sb{i}", tag=("ten0", "ten1", "wide0")[i])
            for n, plan in enumerate(plans[i]):
                copy = nc.vector.tensor_copy if i == last and n % 2 == 0 else nc.scalar.copy
                close_sum(plan, sums[i][n], y_sb[:, n * BANK : (n + 1) * BANK], copy)
            if i == 0:
                sums.append([open_sum(plans[last][0], 0)])
            if i == 1:
                sums[last].extend(open_sum(plan, len(plans[0]) + n) for n, plan in enumerate(plans[last][1:]))
            if i < last:
                for t in range(1, PACK):
                    fetch(zones, i + 1, t)
